import numpy as np
import ml_dtypes


def mxq(x, axis, fmt="e4m3"):
    dtype, down = {"e4m3": (ml_dtypes.float8_e4m3fn, 7), "e5m2": (ml_dtypes.float8_e5m2, 14)}[fmt]
    v = np.moveaxis(np.asarray(x, np.float32).astype(ml_dtypes.bfloat16).astype(np.float64), axis, -1)
    blocks = v.reshape(v.shape[:-1] + (-1, 32))
    amax = np.abs(blocks).max(-1, keepdims=True)
    byte = np.maximum(np.where(amax > 0, np.frexp(amax)[1] - 1 + 127, 0) - down, 1)
    scale = np.exp2(byte - 127.0)
    codes = (blocks / scale).astype(np.float32).astype(dtype).astype(np.float64)
    return np.moveaxis((codes * scale).reshape(v.shape), -1, axis)


WIDE = False


def mx_kscale(k):
    if not WIDE:
        return np.ones(k)
    levels = np.array([10, -10, 5, -5, 0])
    if k % 512:
        return np.exp2(np.random.permutation(np.resize(levels, k // 32))).repeat(32)
    a = np.empty((k // 512, 16))
    for p in range(k // 512):
        a[p, :8] = np.random.permutation(np.resize(levels, 8))
        for g in range(8):
            far = levels[np.abs(levels - a[p, g]) >= 10]
            a[p, g + 8] = far[np.random.randint(len(far))]
    return np.exp2(a.ravel()).repeat(32)


def f64(x):
    return np.asarray(x).astype(np.float64)


def striped(idx):
    return np.tile(idx.reshape(-1, 16).T, (8, 1)).astype(np.uint16)


def unstriped(offs):
    return offs[:16].T.reshape(-1).astype(np.int64)


def gelu(v):
    return 0.5 * v * (1.0 + np.tanh(np.sqrt(2.0 / np.pi) * (v + 0.044715 * v**3)))


K, T, D, S, V, H, N = 1024, 1024, 2, 512, 256, 512, 256


def setup_inputs():
    n = np.random.standard_normal
    s = mx_kscale(K)[:, None]
    u = mx_kscale(H)
    return {
        "xT": (n((K, T)) * s).astype(np.float32),
        "w1": (n((K, H)) / np.sqrt(K) / s * u).astype(np.float32),
        "w2": (n((H, N)) / np.sqrt(H) / u[:, None]).astype(np.float32),
        "gate": np.tile(np.random.uniform(0.5, 1.5, V), (N, 1)).astype(np.float32),
        "offs": striped(np.random.permutation(T)[:S]),
        "pos1": striped(np.random.permutation(2 * V)[:V]),
    }


def reference(xT, w1, w2, gate, offs, pos1):
    h = gelu(mxq(f64(w1), 0, "e4m3").T @ mxq(f64(xT)[:, unstriped(offs)], 0, "e4m3"))
    z = h.reshape(H, V, D).max(axis=2)
    out = np.zeros((N, 2 * V))
    out[:, unstriped(pos1)] = f64(gate) * (mxq(f64(w2), 0, "e4m3").T @ mxq(z, 0, "e4m3"))
    return out

@@ -1,0 +1,206 @@
+from contextlib import ExitStack
+
+import concourse.mybir as mybir
+
+K, T, S, V, H, N = 1024, 1024, 512, 256, 512, 256
+P = 128
+PACK = 4
+K_PASS = P * PACK
+PASSES = K // K_PASS
+
+FLOPS = 2 * K * H * S + 2 * H * N * V
+
+F32 = mybir.dt.float32
+BF16 = mybir.dt.bfloat16
+U32 = mybir.dt.uint32
+U16 = mybir.dt.uint16
+U8 = mybir.dt.uint8
+FP8X4 = mybir.dt.float8_e4m3fn_x4
+MAX = mybir.AluOpType.max
+MULT = mybir.AluOpType.mult
+ADD = mybir.AluOpType.add
+GELU = mybir.ActivationFunctionType.Gelu_apprx_tanh
+
+def interleave(copy, grouped, raw, lo, hi):
+    copy(
+        out=grouped[:, lo:hi, :].rearrange("p (c i) j -> p c j i", i=4),
+        in_=raw[:, :, lo:hi].rearrange("p j (c i) -> p c j i", i=4),
+    )
+
+
+def tile_picked_vpool_gelu_e_kernel(tc, xT, w1, w2, gate, offs, pos1, out):
+    nc = tc.nc
+    scalar_copy = nc.scalar.copy
+    vector_copy = nc.vector.tensor_copy
+    with ExitStack() as ctx:
+        keep = ctx.enter_context(tc.tile_pool(name="keep", bufs=1))
+        psum = ctx.enter_context(tc.psum_pool(name="psum", bufs=1))
+
+        picks = keep.tile([P, S // 16], U16, name="picks")
+        places = keep.tile([P, V // 16], U16, name="places")
+
+        x_scales = keep.tile([P, T], U8, name="x_scales", align_bytes=64)
+        nc.gpsimd.memset(x_scales[:], 0)
+        frames = []
+        for m in range(2):
+            frame = keep.tile([P, 2 * V], F32, name=f"frame{m}", align_bytes=64)
+            nc.gpsimd.memset(frame[:], 0.0)
+            frames.append(frame)
+        warm = keep.tile([P, 8], F32, name="warm")
+        nc.vector.memset(warm[:], 0.0)
+        nc.scalar.activation(warm[:], warm[:], GELU)
+
+        x_raw = {}
+        pieces = (((0, 1024),), ((0, 512), (512, 1024),))
+        for s in range(PASSES):
+            for lo, hi in pieces[s]:
+                raw = keep.tile([P, PACK, hi - lo], F32, name=f"x_raw{s}_{lo}", align_bytes=64)
+                rows = xT[s * K_PASS : (s + 1) * K_PASS, lo:hi]
+                nc.sync.dma_start(out=raw[:], in_=rows.rearrange("(p j) w -> p j w", j=PACK))
+                x_raw[s, lo] = raw
+            if s == 0:
+                nc.sync.dma_start(picks[:], offs)
+        w_raw = []
+        for s in range(PASSES):
+            raw = keep.tile([P, PACK, H], F32, name=f"w_raw{s}", align_bytes=64)
+            rows = w1[s * K_PASS : (s + 1) * K_PASS, :]
+            nc.sync.dma_start(out=raw[:], in_=rows.rearrange("(p j) w -> p j w", j=PACK))
+            w_raw.append(raw)
+        w2_raw = keep.tile([P, PACK, N], F32, name="w2_raw", align_bytes=64)
+        nc.sync.dma_start(out=w2_raw[:], in_=w2.rearrange("(p j) w -> p j w", j=PACK))
+        nc.sync.dma_start(places[:], pos1)
+        gates = keep.tile([P, 2, V], F32, name="gates", align_bytes=64)
+        nc.sync.dma_start(out=gates[:], in_=gate.rearrange("(m p) v -> p m v", p=P))
+
+        x_words = [keep.tile([P, T], U32, name=f"x_words{s}", align_bytes=64) for s in range(PASSES)]
+        picked_words = [keep.tile([P, S], U32, name=f"picked_words{s}", align_bytes=64) for s in range(PASSES)]
+        picked_scales = keep.tile([P, S], U8, name="picked_scales", align_bytes=64)
+        shares = ((432,), (304, 256,))
+        x_grouped = [keep.tile([P, T, PACK], BF16, name=f"x_grouped{s}", align_bytes=64) for s in range(PASSES)]
+
+        def x_copy(s, i):
+            lo, hi = pieces[s][i]
+            part = x_grouped[s][:, lo:hi, :]
+            interleave(scalar_copy, part, x_raw[s, lo], 0, shares[s][i])
+            interleave(vector_copy, part, x_raw[s, lo], shares[s][i], hi - lo)
+
+        def x_quantise(s, lo, hi):
+            nc.vector.quantize_mx(
+                out=x_words[s][:, lo:hi].bitcast(FP8X4),
+                scales=x_scales[4 * s :, lo:hi],
+                in_=x_grouped[s][:, lo:hi, :].rearrange("p w j -> p (w j)"),
+            )
+
+        x_copy(0, 0)
+        x_copy(1, 0)
+        x_quantise(0, 0, T)
+        nc.vector.tensor_copy(picked_words[0][:], x_words[0][:].indirect(picks[:]))
+        x_quantise(1, 0, 512)
+        x_copy(1, 1)
+        x_quantise(1, 512, T)
+        nc.vector.tensor_copy(picked_words[1][:], x_words[1][:].indirect(picks[:]))
+        nc.vector.tensor_copy(picked_scales[:], x_scales[:].indirect(picks[:]))
+
+        w_words = [keep.tile([P, H], U32, name=f"w_words{s}", align_bytes=64) for s in range(PASSES)]
+        w_scales = [keep.tile([P, H], U8, name=f"w_scales{s}", align_bytes=64) for s in range(PASSES)]
+        w_grouped = [keep.tile([P, PACK, P, PACK], BF16, name=f"w_grouped{s}", align_bytes=64) for s in range(PASSES)]
+
+        def regroup(copy, s, lo, hi):
+            copy(
+                out=w_grouped[s][:, :, lo:hi, :].rearrange("p t m j -> p m j t"),
+                in_=w_raw[s][:, :, PACK * lo : PACK * hi].rearrange("p j (m t) -> p m j t", t=PACK),
+            )
+
+        def w_quantise(s, lo, hi):
+            nc.vector.quantize_mx(
+                out=w_words[s][:, lo * P : hi * P].bitcast(FP8X4),
+                scales=w_scales[s][:, lo * P : hi * P],
+                in_=w_grouped[s][:, lo:hi, :, :].rearrange("p t m j -> p (t m j)"),
+            )
+
+        def pool_copy(out, in_):
+            nc.gpsimd.tensor_scalar(out, in_, 1.0, 0.0, MULT, ADD)
+
+        regroup(scalar_copy, 0, 0, 128)
+
+        w_quantise(0, 0, PACK)
+        hidden = []
+        banks = {}
+
+        def product(half, pair, u, s):
+            t = 2 * pair + u
+            cols = slice(half * V, (half + 1) * V)
+            nc.tensor.matmul_mx(
+                out=banks[half, pair][:, u, :],
+                lhsT=w_words[s][:, t * P : (t + 1) * P].bitcast(FP8X4),
+                lhsT_scale=w_scales[s][:, t * P : (t + 1) * P],
+                rhs=picked_words[s][:, cols].bitcast(FP8X4),
+                rhs_scale=picked_scales[4 * s :, cols],
+                start=(s == 0),
+                stop=(s == PASSES - 1),
+            )
+
+        for half in range(2):
+            for pair in range(2):
+                banks[half, pair] = psum.tile([P, 2, V], F32, name=f"bank{half}{pair}")
+                product(half, pair, 0, 0)
+        regroup(vector_copy, 1, 0, 72)
+        regroup(scalar_copy, 1, 72, P)
+        for t in range(PACK):
+            w_quantise(1, t, t + 1)
+
+        for half, pair in ((0, 0), (0, 1), (1, 0), (1, 1)):
+            if pair == 0:
+                hidden.append(keep.tile([P, PACK, V], F32, name=f"hidden{half}", align_bytes=64))
+            product(half, pair, 0, 1)
+            product(half, pair, 1, 0)
+            product(half, pair, 1, 1)
+            nc.scalar.activation(hidden[half][:, 2 * pair : 2 * pair + 2, :], banks[half, pair][:], GELU)
+
+        w2_grouped = keep.tile([P, N, PACK], BF16, name="w2_grouped", align_bytes=64)
+        interleave(vector_copy, w2_grouped[:], w2_raw, 0, N)
+        w2_words = keep.tile([P, N], U32, name="w2_words", align_bytes=64)
+        w2_scales = keep.tile([P, N], U8, name="w2_scales", align_bytes=64)
+        nc.vector.quantize_mx(
+            out=w2_words[:].bitcast(FP8X4), scales=w2_scales[:], in_=w2_grouped[:].rearrange("p w j -> p (w j)")
+        )
+
+        HV = V // 2
+        results = []
+        for half in range(2):
+            pooled = keep.tile([P, HV, PACK], BF16, name=f"pooled{half}", align_bytes=64)
+            pairs = hidden[half][:].rearrange("p t (c i d) -> p c t i d", i=4, d=2)
+            nc.vector.tensor_tensor(
+                pooled[:].rearrange("p (c i) t -> p c t i", i=4),
+                pairs[:, :, :, :, 0],
+                pairs[:, :, :, :, 1],
+                MAX,
+            )
+            z_words = keep.tile([P, HV], U32, name=f"z_words{half}", align_bytes=64)
+            z_scales = keep.tile([P, HV], U8, name=f"z_scales{half}", align_bytes=64)
+            nc.vector.quantize_mx(
+                out=z_words[:].bitcast(FP8X4), scales=z_scales[:], in_=pooled[:].rearrange("p w j -> p (w j)")
+            )
+            bank = psum.tile([P, 2, HV], F32, name=f"out_bank{half}")
+            for m in range(2):
+                nc.tensor.matmul_mx(
+                    out=bank[:, m, :],
+                    lhsT=w2_words[:, m * P : (m + 1) * P].bitcast(FP8X4),
+                    lhsT_scale=w2_scales[:, m * P : (m + 1) * P],
+                    rhs=z_words[:].bitcast(FP8X4),
+                    rhs_scale=z_scales[:],
+                    start=True,
+                    stop=True,
+                )
+            result = keep.tile([P, 2, HV], F32, name=f"result{half}", align_bytes=64)
+            nc.scalar.copy(out=result[:], in_=bank[:])
+            results.append(result)
+        for m, half in ((0, 0), (0, 1), (1, 0), (1, 1)):
+            nc.vector.tensor_tensor(
+                frames[m][:].indirect(places[:, half * 8 : half * 8 + 8]),
+                results[half][:, m, :],
+                gates[:, m, half * HV : (half + 1) * HV],
+                MULT,
+            )
+            if half == 1:
+                nc.sync.dma_start(out=out[m * P : (m + 1) * P, :], in_=frames[m][:])

@@ -7,6 +7,8 @@ P = 128
 PACK = 4
 K_PASS = P * PACK
 PASSES = K // K_PASS
+HS = S // 2
+HV = V // 2
 
 FLOPS = 2 * K * H * S + 2 * H * N * V
 
@@ -18,29 +20,23 @@ U8 = mybir.dt.uint8
 FP8X4 = mybir.dt.float8_e4m3fn_x4
 MAX = mybir.AluOpType.max
 MULT = mybir.AluOpType.mult
-ADD = mybir.AluOpType.add
 GELU = mybir.ActivationFunctionType.Gelu_apprx_tanh
+COPY = mybir.ActivationFunctionType.Copy
 
-def interleave(copy, grouped, raw, lo, hi):
-    copy(
-        out=grouped[:, lo:hi, :].rearrange("p (c i) j -> p c j i", i=4),
-        in_=raw[:, :, lo:hi].rearrange("p j (c i) -> p c j i", i=4),
-    )
+SCALAR_PLANES = ((1, 0), (1, 1))
 
 
 def tile_picked_vpool_gelu_e_kernel(tc, xT, w1, w2, gate, offs, pos1, out):
     nc = tc.nc
     scalar_copy = nc.scalar.copy
     vector_copy = nc.vector.tensor_copy
+
     with ExitStack() as ctx:
         keep = ctx.enter_context(tc.tile_pool(name="keep", bufs=1))
         psum = ctx.enter_context(tc.psum_pool(name="psum", bufs=1))
 
         picks = keep.tile([P, S // 16], U16, name="picks")
         places = keep.tile([P, V // 16], U16, name="places")
-
-        x_scales = keep.tile([P, T], U8, name="x_scales", align_bytes=64)
-        nc.gpsimd.memset(x_scales[:], 0)
         frames = []
         for m in range(2):
             frame = keep.tile([P, 2 * V], F32, name=f"frame{m}", align_bytes=64)
@@ -50,16 +46,14 @@ def tile_picked_vpool_gelu_e_kernel(tc, xT, w1, w2, gate, offs, pos1, out):
         nc.vector.memset(warm[:], 0.0)
         nc.scalar.activation(warm[:], warm[:], GELU)
 
+        nc.sync.dma_start(picks[:], offs)
         x_raw = {}
-        pieces = (((0, 1024),), ((0, 512), (512, 1024),))
         for s in range(PASSES):
-            for lo, hi in pieces[s]:
-                raw = keep.tile([P, PACK, hi - lo], F32, name=f"x_raw{s}_{lo}", align_bytes=64)
-                rows = xT[s * K_PASS : (s + 1) * K_PASS, lo:hi]
-                nc.sync.dma_start(out=raw[:], in_=rows.rearrange("(p j) w -> p j w", j=PACK))
-                x_raw[s, lo] = raw
-            if s == 0:
-                nc.sync.dma_start(picks[:], offs)
+            rows = xT[s * K_PASS : (s + 1) * K_PASS, :].rearrange("(p j) w -> p j w", j=PACK)
+            for j in range(PACK):
+                raw = keep.tile([P, T], F32, name=f"x_raw{s}{j}", align_bytes=64)
+                nc.sync.dma_start(out=raw[:], in_=rows[:, j, :])
+                x_raw[s, j] = raw
         w_raw = []
         for s in range(PASSES):
             raw = keep.tile([P, PACK, H], F32, name=f"w_raw{s}", align_bytes=64)
@@ -72,34 +66,24 @@ def tile_picked_vpool_gelu_e_kernel(tc, xT, w1, w2, gate, offs, pos1, out):
         gates = keep.tile([P, 2, V], F32, name="gates", align_bytes=64)
         nc.sync.dma_start(out=gates[:], in_=gate.rearrange("(m p) v -> p m v", p=P))
 
-        x_words = [keep.tile([P, T], U32, name=f"x_words{s}", align_bytes=64) for s in range(PASSES)]
-        picked_words = [keep.tile([P, S], U32, name=f"picked_words{s}", align_bytes=64) for s in range(PASSES)]
-        picked_scales = keep.tile([P, S], U8, name="picked_scales", align_bytes=64)
-        shares = ((432,), (304, 256,))
-        x_grouped = [keep.tile([P, T, PACK], BF16, name=f"x_grouped{s}", align_bytes=64) for s in range(PASSES)]
-
-        def x_copy(s, i):
-            lo, hi = pieces[s][i]
-            part = x_grouped[s][:, lo:hi, :]
-            interleave(scalar_copy, part, x_raw[s, lo], 0, shares[s][i])
-            interleave(vector_copy, part, x_raw[s, lo], shares[s][i], hi - lo)
-
-        def x_quantise(s, lo, hi):
+        x_words = []
+        x_scales = []
+        for s in range(PASSES):
+            grouped = keep.tile([P, S, PACK], BF16, name=f"x_grouped{s}", align_bytes=64)
+            for j in range(PACK):
+                if (s, j) in SCALAR_PLANES:
+                    rounded = keep.tile([P, T], BF16, name=f"x_rounded{s}{j}", align_bytes=64)
+                    nc.scalar.copy(out=rounded[:], in_=x_raw[s, j][:])
+                    nc.scalar.activation(grouped[:, :, j], rounded[:].indirect(picks[:]), COPY)
+                else:
+                    nc.vector.tensor_copy(grouped[:, :, j], x_raw[s, j][:].indirect(picks[:]))
+            words = keep.tile([P, S], U32, name=f"x_words{s}", align_bytes=64)
+            scales = keep.tile([P, S], U8, name=f"x_scales{s}", align_bytes=64)
             nc.vector.quantize_mx(
-                out=x_words[s][:, lo:hi].bitcast(FP8X4),
-                scales=x_scales[4 * s :, lo:hi],
-                in_=x_grouped[s][:, lo:hi, :].rearrange("p w j -> p (w j)"),
+                out=words[:].bitcast(FP8X4), scales=scales[:], in_=grouped[:].rearrange("p n j -> p (n j)")
             )
-
-        x_copy(0, 0)
-        x_copy(1, 0)
-        x_quantise(0, 0, T)
-        nc.vector.tensor_copy(picked_words[0][:], x_words[0][:].indirect(picks[:]))
-        x_quantise(1, 0, 512)
-        x_copy(1, 1)
-        x_quantise(1, 512, T)
-        nc.vector.tensor_copy(picked_words[1][:], x_words[1][:].indirect(picks[:]))
-        nc.vector.tensor_copy(picked_scales[:], x_scales[:].indirect(picks[:]))
+            x_words.append(words)
+            x_scales.append(scales)
 
         w_words = [keep.tile([P, H], U32, name=f"w_words{s}", align_bytes=64) for s in range(PASSES)]
         w_scales = [keep.tile([P, H], U8, name=f"w_scales{s}", align_bytes=64) for s in range(PASSES)]
@@ -118,54 +102,50 @@ def tile_picked_vpool_gelu_e_kernel(tc, xT, w1, w2, gate, offs, pos1, out):
                 in_=w_grouped[s][:, lo:hi, :, :].rearrange("p t m j -> p (t m j)"),
             )
 
-        def pool_copy(out, in_):
-            nc.gpsimd.tensor_scalar(out, in_, 1.0, 0.0, MULT, ADD)
-
-        regroup(scalar_copy, 0, 0, 128)
-
+        regroup(scalar_copy, 0, 0, 88)
+        regroup(vector_copy, 0, 88, P)
         w_quantise(0, 0, PACK)
-        hidden = []
         banks = {}
+        hidden = [keep.tile([P, PACK, HS], F32, name=f"hidden{h}", align_bytes=64) for h in range(2)]
 
-        def product(half, pair, u, s):
-            t = 2 * pair + u
-            cols = slice(half * V, (half + 1) * V)
+        def product(half, t, s):
+            cols = slice(half * HS, (half + 1) * HS)
             nc.tensor.matmul_mx(
-                out=banks[half, pair][:, u, :],
+                out=banks[half, t // 2][:, t % 2, :],
                 lhsT=w_words[s][:, t * P : (t + 1) * P].bitcast(FP8X4),
                 lhsT_scale=w_scales[s][:, t * P : (t + 1) * P],
-                rhs=picked_words[s][:, cols].bitcast(FP8X4),
-                rhs_scale=picked_scales[4 * s :, cols],
+                rhs=x_words[s][:, cols].bitcast(FP8X4),
+                rhs_scale=x_scales[s][:, cols],
                 start=(s == 0),
                 stop=(s == PASSES - 1),
             )
 
         for half in range(2):
             for pair in range(2):
-                banks[half, pair] = psum.tile([P, 2, V], F32, name=f"bank{half}{pair}")
-                product(half, pair, 0, 0)
+                banks[half, pair] = psum.tile([P, 2, HS], F32, name=f"bank{half}{pair}")
+                product(half, 2 * pair, 0)
         regroup(vector_copy, 1, 0, 72)
         regroup(scalar_copy, 1, 72, P)
         for t in range(PACK):
             w_quantise(1, t, t + 1)
 
         for half, pair in ((0, 0), (0, 1), (1, 0), (1, 1)):
-            if pair == 0:
-                hidden.append(keep.tile([P, PACK, V], F32, name=f"hidden{half}", align_bytes=64))
-            product(half, pair, 0, 1)
-            product(half, pair, 1, 0)
-            product(half, pair, 1, 1)
+            product(half, 2 * pair, 1)
+            product(half, 2 * pair + 1, 0)
+            product(half, 2 * pair + 1, 1)
             nc.scalar.activation(hidden[half][:, 2 * pair : 2 * pair + 2, :], banks[half, pair][:], GELU)
 
         w2_grouped = keep.tile([P, N, PACK], BF16, name="w2_grouped", align_bytes=64)
-        interleave(vector_copy, w2_grouped[:], w2_raw, 0, N)
+        vector_copy(
+            out=w2_grouped[:].rearrange("p (c i) j -> p c j i", i=4),
+            in_=w2_raw[:].rearrange("p j (c i) -> p c j i", i=4),
+        )
         w2_words = keep.tile([P, N], U32, name="w2_words", align_bytes=64)
         w2_scales = keep.tile([P, N], U8, name="w2_scales", align_bytes=64)
         nc.vector.quantize_mx(
             out=w2_words[:].bitcast(FP8X4), scales=w2_scales[:], in_=w2_grouped[:].rearrange("p w j -> p (w j)")
         )
 
-        HV = V // 2
         results = []
         for half in range(2):
             pooled = keep.tile([P, HV, PACK], BF16, name=f"pooled{half}", align_bytes=64)

from contextlib import ExitStack

import concourse.mybir as mybir

K, T, S, V, H, N = 1024, 1024, 512, 256, 512, 256
P = 128
PACK = 4
K_PASS = P * PACK
PASSES = K // K_PASS
HS = S // 2
HV = V // 2

FLOPS = 2 * K * H * S + 2 * H * N * V

F32 = mybir.dt.float32
BF16 = mybir.dt.bfloat16
U32 = mybir.dt.uint32
U16 = mybir.dt.uint16
U8 = mybir.dt.uint8
FP8X4 = mybir.dt.float8_e4m3fn_x4
MAX = mybir.AluOpType.max
MULT = mybir.AluOpType.mult
GELU = mybir.ActivationFunctionType.Gelu_apprx_tanh
COPY = mybir.ActivationFunctionType.Copy

SCALAR_PLANES = ((1, 0), (1, 1))


def tile_picked_vpool_gelu_e_kernel(tc, xT, w1, w2, gate, offs, pos1, out):
    nc = tc.nc
    scalar_copy = nc.scalar.copy
    vector_copy = nc.vector.tensor_copy

    with ExitStack() as ctx:
        keep = ctx.enter_context(tc.tile_pool(name="keep", bufs=1))
        psum = ctx.enter_context(tc.psum_pool(name="psum", bufs=1))

        picks = keep.tile([P, S // 16], U16, name="picks")
        places = keep.tile([P, V // 16], U16, name="places")
        frames = []
        for m in range(2):
            frame = keep.tile([P, 2 * V], F32, name=f"frame{m}", align_bytes=64)
            nc.gpsimd.memset(frame[:], 0.0)
            frames.append(frame)
        warm = keep.tile([P, 8], F32, name="warm")
        nc.vector.memset(warm[:], 0.0)
        nc.scalar.activation(warm[:], warm[:], GELU)

        nc.sync.dma_start(picks[:], offs)
        x_raw = {}
        for s in range(PASSES):
            rows = xT[s * K_PASS : (s + 1) * K_PASS, :].rearrange("(p j) w -> p j w", j=PACK)
            for j in range(PACK):
                raw = keep.tile([P, T], F32, name=f"x_raw{s}{j}", align_bytes=64)
                nc.sync.dma_start(out=raw[:], in_=rows[:, j, :])
                x_raw[s, j] = raw
        w_raw = []
        for s in range(PASSES):
            raw = keep.tile([P, PACK, H], F32, name=f"w_raw{s}", align_bytes=64)
            rows = w1[s * K_PASS : (s + 1) * K_PASS, :]
            nc.sync.dma_start(out=raw[:], in_=rows.rearrange("(p j) w -> p j w", j=PACK))
            w_raw.append(raw)
        w2_raw = keep.tile([P, PACK, N], F32, name="w2_raw", align_bytes=64)
        nc.sync.dma_start(out=w2_raw[:], in_=w2.rearrange("(p j) w -> p j w", j=PACK))
        nc.sync.dma_start(places[:], pos1)
        gates = keep.tile([P, 2, V], F32, name="gates", align_bytes=64)
        nc.sync.dma_start(out=gates[:], in_=gate.rearrange("(m p) v -> p m v", p=P))

        x_words = []
        x_scales = []
        for s in range(PASSES):
            grouped = keep.tile([P, S, PACK], BF16, name=f"x_grouped{s}", align_bytes=64)
            for j in range(PACK):
                if (s, j) in SCALAR_PLANES:
                    rounded = keep.tile([P, T], BF16, name=f"x_rounded{s}{j}", align_bytes=64)
                    nc.scalar.copy(out=rounded[:], in_=x_raw[s, j][:])
                    nc.scalar.activation(grouped[:, :, j], rounded[:].indirect(picks[:]), COPY)
                else:
                    nc.vector.tensor_copy(grouped[:, :, j], x_raw[s, j][:].indirect(picks[:]))
            words = keep.tile([P, S], U32, name=f"x_words{s}", align_bytes=64)
            scales = keep.tile([P, S], U8, name=f"x_scales{s}", align_bytes=64)
            nc.vector.quantize_mx(
                out=words[:].bitcast(FP8X4), scales=scales[:], in_=grouped[:].rearrange("p n j -> p (n j)")
            )
            x_words.append(words)
            x_scales.append(scales)

        w_words = [keep.tile([P, H], U32, name=f"w_words{s}", align_bytes=64) for s in range(PASSES)]
        w_scales = [keep.tile([P, H], U8, name=f"w_scales{s}", align_bytes=64) for s in range(PASSES)]
        w_grouped = [keep.tile([P, PACK, P, PACK], BF16, name=f"w_grouped{s}", align_bytes=64) for s in range(PASSES)]

        def regroup(copy, s, lo, hi):
            copy(
                out=w_grouped[s][:, :, lo:hi, :].rearrange("p t m j -> p m j t"),
                in_=w_raw[s][:, :, PACK * lo : PACK * hi].rearrange("p j (m t) -> p m j t", t=PACK),
            )

        def w_quantise(s, lo, hi):
            nc.vector.quantize_mx(
                out=w_words[s][:, lo * P : hi * P].bitcast(FP8X4),
                scales=w_scales[s][:, lo * P : hi * P],
                in_=w_grouped[s][:, lo:hi, :, :].rearrange("p t m j -> p (t m j)"),
            )

        regroup(scalar_copy, 0, 0, 88)
        regroup(vector_copy, 0, 88, P)
        w_quantise(0, 0, PACK)
        banks = {}
        hidden = [keep.tile([P, PACK, HS], F32, name=f"hidden{h}", align_bytes=64) for h in range(2)]

        def product(half, t, s):
            cols = slice(half * HS, (half + 1) * HS)
            nc.tensor.matmul_mx(
                out=banks[half, t // 2][:, t % 2, :],
                lhsT=w_words[s][:, t * P : (t + 1) * P].bitcast(FP8X4),
                lhsT_scale=w_scales[s][:, t * P : (t + 1) * P],
                rhs=x_words[s][:, cols].bitcast(FP8X4),
                rhs_scale=x_scales[s][:, cols],
                start=(s == 0),
                stop=(s == PASSES - 1),
            )

        for half in range(2):
            for pair in range(2):
                banks[half, pair] = psum.tile([P, 2, HS], F32, name=f"bank{half}{pair}")
                product(half, 2 * pair, 0)
        regroup(vector_copy, 1, 0, 72)
        regroup(scalar_copy, 1, 72, P)
        for t in range(PACK):
            w_quantise(1, t, t + 1)

        for half, pair in ((0, 0), (0, 1), (1, 0), (1, 1)):
            product(half, 2 * pair, 1)
            product(half, 2 * pair + 1, 0)
            product(half, 2 * pair + 1, 1)
            nc.scalar.activation(hidden[half][:, 2 * pair : 2 * pair + 2, :], banks[half, pair][:], GELU)

        w2_grouped = keep.tile([P, N, PACK], BF16, name="w2_grouped", align_bytes=64)
        vector_copy(
            out=w2_grouped[:].rearrange("p (c i) j -> p c j i", i=4),
            in_=w2_raw[:].rearrange("p j (c i) -> p c j i", i=4),
        )
        w2_words = keep.tile([P, N], U32, name="w2_words", align_bytes=64)
        w2_scales = keep.tile([P, N], U8, name="w2_scales", align_bytes=64)
        nc.vector.quantize_mx(
            out=w2_words[:].bitcast(FP8X4), scales=w2_scales[:], in_=w2_grouped[:].rearrange("p w j -> p (w j)")
        )

        results = []
        for half in range(2):
            pooled = keep.tile([P, HV, PACK], BF16, name=f"pooled{half}", align_bytes=64)
            pairs = hidden[half][:].rearrange("p t (c i d) -> p c t i d", i=4, d=2)
            nc.vector.tensor_tensor(
                pooled[:].rearrange("p (c i) t -> p c t i", i=4),
                pairs[:, :, :, :, 0],
                pairs[:, :, :, :, 1],
                MAX,
            )
            z_words = keep.tile([P, HV], U32, name=f"z_words{half}", align_bytes=64)
            z_scales = keep.tile([P, HV], U8, name=f"z_scales{half}", align_bytes=64)
            nc.vector.quantize_mx(
                out=z_words[:].bitcast(FP8X4), scales=z_scales[:], in_=pooled[:].rearrange("p w j -> p (w j)")
            )
            bank = psum.tile([P, 2, HV], F32, name=f"out_bank{half}")
            for m in range(2):
                nc.tensor.matmul_mx(
                    out=bank[:, m, :],
                    lhsT=w2_words[:, m * P : (m + 1) * P].bitcast(FP8X4),
                    lhsT_scale=w2_scales[:, m * P : (m + 1) * P],
                    rhs=z_words[:].bitcast(FP8X4),
                    rhs_scale=z_scales[:],
                    start=True,
                    stop=True,
                )
            result = keep.tile([P, 2, HV], F32, name=f"result{half}", align_bytes=64)
            nc.scalar.copy(out=result[:], in_=bank[:])
            results.append(result)
        for m, half in ((0, 0), (0, 1), (1, 0), (1, 1)):
            nc.vector.tensor_tensor(
                frames[m][:].indirect(places[:, half * 8 : half * 8 + 8]),
                results[half][:, m, :],
                gates[:, m, half * HV : (half + 1) * HV],
                MULT,
            )
            if half == 1:
                nc.sync.dma_start(out=out[m * P : (m + 1) * P, :], in_=frames[m][:])
